import numpy as np, ml_dtypes
CORES = [113,118,241,246]
N = 4
DEG, TK, TIMES = 3, 512, 3
MASK = [[3,0,1],[0,1,2],[1,2,3],[2,3,0]]
def setup_inputs(rng):
    return {"x": rng.standard_normal((N, 128, TK), dtype=np.float32).astype(ml_dtypes.bfloat16), "w": (rng.standard_normal((N, 128, DEG * 128), dtype=np.float32) / np.float32(np.sqrt(128 * DEG / 2))).astype(ml_dtypes.bfloat16)}
def setup_inputs_big(rng):
    d = setup_inputs(rng)
    for k in ("x",): d[k] = (d[k].astype(np.float32) * 1048576.0).astype(d[k].dtype)
    return d
def setup_inputs_small(rng):
    d = setup_inputs(rng)
    for k in ("x",): d[k] = (d[k].astype(np.float32) * (1 / 1048576.0)).astype(d[k].dtype)
    return d
def setup_inputs_apart(rng):
    d = setup_inputs(rng)
    f = (10.0 ** rng.permutation(np.linspace(-1.5, 1.5, N))).astype(np.float32).reshape(N, 1, 1)
    for k in ("x",): d[k] = (d[k].astype(np.float32) * f).astype(d[k].dtype)
    return d
def reference(x, w):
    X, W = x.astype(np.float64), w.astype(np.float64)
    h = list(X)
    for _ in range(TIMES):
        h = [sum(W[r][:, 128 * i:128 * i + 128].T @ h[j] for i, j in enumerate(MASK[r])) for r in range(N)]
    return {"y": np.stack(h).astype(ml_dtypes.bfloat16)}

@@ -1,0 +1,213 @@
+from concourse.bass import DstId, RemoteDMATransfer
+
+N, DEG, P, TK = 4, 3, 128, 512
+WC = DEG * P
+NH = 2
+HW = TK // NH
+
+SCRATCH = {
+    "wb": ("sbuf", [P, N * WC], "bfloat16"),
+    "xb": ("sbuf", [P, N * TK], "bfloat16"),
+    "wt": ("sbuf", [P, N * WC], "bfloat16"),
+    "v2": ("sbuf", [P, N * P], "bfloat16"),
+    "v3": ("sbuf", [P, N * P], "bfloat16"),
+    "ys": ("sbuf", [P, TK], "bfloat16"),
+    "z": ("sbuf", [P, P + 1], "bfloat16"),
+    "idn": ("sbuf", [P, P], "bfloat16"),
+    "idd": ("dram", [1, P * (P + 1)], "bfloat16"),
+    "tra": ("psum", [P, 512], "float32"),
+    "trb": ("psum", [P, 512], "float32"),
+    "p0": ("psum", [P, 512], "float32"),
+    "p1": ("psum", [P, 512], "float32"),
+    "p2": ("psum", [P, 512], "float32"),
+    "p3": ("psum", [P, 512], "float32"),
+    "y0": ("psum", [P, 512], "float32"),
+    "y1": ("psum", [P, 512], "float32"),
+}
+SEMAPHORES = (["wl", "xl", "ms", "idw", "idr", "sent"]
+              + ["%s%d" % (s, k) for s in ("wa", "xa", "tr", "wt", "v2m", "v2c", "v3m", "v3c") for k in range(N)]
+              + ["%s%d" % (s, h) for s in ("ym", "yc", "st") for h in range(NH)])
+
+
+def _bits(m):
+    return [b for b in range(m.bit_length()) if (m >> b) & 1]
+
+
+def _mask_of(bs):
+    m = 0
+    for b in bs:
+        m |= 1 << b
+    return m
+
+
+def _share(engines, parts):
+    per = len(engines) // parts
+    per = 1 << (per.bit_length() - 1)
+    return [_mask_of(engines[t * per:(t + 1) * per]) for t in range(parts)]
+
+
+def _same_chip(topo, a, b):
+    return topo.host(a) == topo.host(b) and topo.chip(a) == topo.chip(b)
+
+
+def _plan(topo, cores, src):
+    c = cores[src]
+    near = [j for j in range(len(cores)) if j != src and _same_chip(topo, cores[j], c)]
+    far = [j for j in range(len(cores)) if j != src and not _same_chip(topo, cores[j], c)]
+    masks = {}
+    off = 0
+    if far:
+        off = topo.mask(c, cores[far[0]])
+        for j in far:
+            off &= topo.mask(c, cores[j])
+        for j, m in zip(far, _share(_bits(off), len(far))):
+            masks[j] = m
+    if near:
+        on = topo.mask(c, cores[near[0]])
+        for j in near:
+            on &= topo.mask(c, cores[j])
+        rest = on & ~off
+        for j, m in zip(near, _share(_bits(rest if rest else on), len(near))):
+            masks[j] = m
+    return near, far, masks
+
+
+def rank_program(g, core, T, topo):
+    r = T.rank_of(core)
+    if r is None:
+        return
+    MASK, cores, S = T.tables["MASK"], T.cores, T.sem
+    pe, ve, sy, sc = g.tensor, g.vector, g.sync, g.scalar
+    near, far, mine = _plan(topo, cores, r)
+    order = [r] + near + sorted(far, key=lambda j: 0 if j in MASK[r] else 1)
+
+    def engines(src):
+        return len(_bits(_plan(topo, cores, src)[2][r]))
+
+    def wtile(buf, k, i):
+        return buf[:, k * WC + i * P:k * WC + (i + 1) * P]
+
+    def blk(buf, j):
+        return buf[:, j * P:(j + 1) * P]
+
+    sy.dma_start(T.wb[:, r * WC:(r + 1) * WC], T.w[:]).then_inc(S.wl, 16)
+    sy.dma_start(T.xb[:, r * TK:(r + 1) * TK], T.x[:]).then_inc(S.xl, 16)
+    ve.memset(T.z[:], 0.0).then_inc(S.ms, 1)
+    ve.wait_ge(S.ms, 1)
+    ve.memset(T.z[:, 0:1], 1.0).then_inc(S.ms, 1)
+    sc.wait_ge(S.ms, 2)
+    sc.dma_start(T.idd[0], T.z[:]).then_inc(S.idw, 16)
+    sc.wait_ge(S.idw, 16)
+    sc.dma_start(T.idn[:], T.idd[0, 0:P * P]).then_inc(S.idr, 16)
+
+    sent = [0]
+
+    def send(dsts, buf, width, sem):
+        if not dsts:
+            return
+        ap = buf[:, r * width:(r + 1) * width]
+        trs = []
+        for j in dsts:
+            rid, pid = topo.addr(cores[j], core)
+            trs.append(RemoteDMATransfer(dst_ids=[DstId(rid=rid, pnc=pid)], dma_engine_mask=mine[j], remote_sem=sem,
+                                         src=ap, dst=ap))
+            sent[0] += len(_bits(mine[j]))
+        g.remote_dma_fused(trs, local_sem=S.sent)
+
+    g.wait_ge(S.wl, 16)
+    send(far, T.wb, WC, S["wa%d" % r])
+    send(near, T.wb, WC, S["wa%d" % r])
+    g.wait_ge(S.xl, 16)
+    send(far, T.xb, TK, S["xa%d" % r])
+    send(near, T.xb, TK, S["xa%d" % r])
+    g.wait_ge(S.sent, sent[0])
+
+    t2 = [(MASK[k][i2], k, i1, i2) for k in order for i1 in range(DEG) if MASK[r][i1] == k for i2 in range(DEG)]
+    n2 = [sum(1 for t in t2 if t[0] == j) for j in range(N)]
+    t3 = {j: [(l, i) for l in order if n2[l] for i in range(DEG) if MASK[l][i] == j] for j in range(N)}
+    last2 = {t[0]: t[1] for t in t2}
+    early = order[:1 + len(near)]
+    bank = {k: (T.tra, T.trb)[n % 2] for n, k in enumerate(order)}
+
+    def have_w(k):
+        if k == r:
+            pe.wait_ge(S.wl, 16)
+        else:
+            pe.wait_ge(S["wa%d" % k], engines(k))
+
+    def have_x(j):
+        if j == r:
+            pe.wait_ge(S.xl, 16)
+        else:
+            pe.wait_ge(S["xa%d" % j], engines(j))
+
+    def transpose(k):
+        have_w(k)
+        for i in range(DEG):
+            pe.matmul(out=blk(bank[k], i), lhsT=wtile(T.wb, k, i), rhs=T.idn[:], start=True, stop=True
+                      ).then_inc(S["tr%d" % k], 1)
+
+    seen2 = [0] * N
+
+    def v2_terms(k):
+        pe.wait_ge(S["wt%d" % k], 1)
+        for (j, kk, i1, i2) in t2:
+            if kk != k:
+                continue
+            seen2[j] += 1
+            pe.matmul(out=blk(T["p%d" % j], 0), lhsT=wtile(T.wt, k, i2), rhs=wtile(T.wb, r, i1),
+                      start=(seen2[j] == 1), stop=(seen2[j] == n2[j])).then_inc(S["v2m%d" % j], 1)
+
+    pe.wait_ge(S.idr, 16)
+    for k in early:
+        transpose(k)
+    for k in early:
+        v2_terms(k)
+    for k in order[len(early):]:
+        transpose(k)
+    for k in order[len(early):]:
+        v2_terms(k)
+    for j in range(N):
+        if n2[j]:
+            pe.wait_ge(S["v2c%d" % j], 1)
+    for j in order:
+        for n, (l, i) in enumerate(t3[j]):
+            pe.matmul(out=blk(T["p%d" % j], 0), lhsT=wtile(T.wt, l, i), rhs=blk(T.v2, l),
+                      start=(n == 0), stop=(n == len(t3[j]) - 1)).then_inc(S["v3m%d" % j], 1)
+    for n, j in enumerate(order):
+        pe.wait_ge(S["v3c%d" % j], 1)
+        have_x(j)
+        for h in range(NH):
+            pe.matmul(out=T["y%d" % h][:, 0:HW], lhsT=blk(T.v3, j), rhs=T.xb[:, j * TK + h * HW:j * TK + (h + 1) * HW],
+                      start=(n == 0), stop=(n == N - 1)).then_inc(S["ym%d" % h], 1)
+
+    def wt_copy(k):
+        ve.wait_ge(S["tr%d" % k], DEG)
+        ve.tensor_copy(out=T.wt[:, k * WC:(k + 1) * WC], in_=bank[k][:, 0:WC]).then_inc(S["wt%d" % k], 1)
+
+    def v2_copy(j):
+        ve.wait_ge(S["v2m%d" % j], n2[j])
+        ve.tensor_copy(out=blk(T.v2, j), in_=blk(T["p%d" % j], 0)).then_inc(S["v2c%d" % j], 1)
+
+    for k in early:
+        wt_copy(k)
+    for j in order:
+        if n2[j] and last2[j] in early:
+            v2_copy(j)
+    for k in order[len(early):]:
+        wt_copy(k)
+    for j in order:
+        if n2[j] and last2[j] not in early:
+            v2_copy(j)
+    for j in order:
+        ve.wait_ge(S["v3m%d" % j], len(t3[j]))
+        ve.tensor_copy(out=blk(T.v3, j), in_=blk(T["p%d" % j], 0)).then_inc(S["v3c%d" % j], 1)
+    for h in range(NH):
+        ve.wait_ge(S["ym%d" % h], N)
+        ve.tensor_copy(out=T.ys[:, h * HW:(h + 1) * HW], in_=T["y%d" % h][:, 0:HW]).then_inc(S["yc%d" % h], 1)
+
+    for h in range(NH):
+        q = (sy, sc)[h % 2]
+        q.wait_ge(S["yc%d" % h], 1)
+        q.dma_start(T.y[:, h * HW:(h + 1) * HW], T.ys[:, h * HW:(h + 1) * HW]).then_inc(S["st%d" % h], 16)
+        q.wait_ge(S["st%d" % h], 16)

@@ -1,9 +1,10 @@
 from concourse.bass import DstId, RemoteDMATransfer
+from concourse.mybir import AluOpType, ActivationFunctionType
 
 N, DEG, P, TK = 4, 3, 128, 512
 WC = DEG * P
-NH = 2
-HW = TK // NH
+NQ = TK // P
+NBANK = 8
 
 SCRATCH = {
     "wb": ("sbuf", [P, N * WC], "bfloat16"),
@@ -12,64 +13,56 @@ SCRATCH = {
     "v2": ("sbuf", [P, N * P], "bfloat16"),
     "v3": ("sbuf", [P, N * P], "bfloat16"),
     "ys": ("sbuf", [P, TK], "bfloat16"),
-    "z": ("sbuf", [P, P + 1], "bfloat16"),
+    "one": ("sbuf", [P, P], "bfloat16"),
     "idn": ("sbuf", [P, P], "bfloat16"),
-    "idd": ("dram", [1, P * (P + 1)], "bfloat16"),
-    "tra": ("psum", [P, 512], "float32"),
-    "trb": ("psum", [P, 512], "float32"),
-    "p0": ("psum", [P, 512], "float32"),
-    "p1": ("psum", [P, 512], "float32"),
-    "p2": ("psum", [P, 512], "float32"),
-    "p3": ("psum", [P, 512], "float32"),
-    "y0": ("psum", [P, 512], "float32"),
-    "y1": ("psum", [P, 512], "float32"),
 }
-SEMAPHORES = (["wl", "xl", "ms", "idw", "idr", "sent"]
-              + ["%s%d" % (s, k) for s in ("wa", "xa", "tr", "wt", "v2m", "v2c", "v3m", "v3c") for k in range(N)]
-              + ["%s%d" % (s, h) for s in ("ym", "yc", "st") for h in range(NH)])
+for _n in range(NBANK):
+    SCRATCH["k%d" % _n] = ("psum", [P, 512], "float32")
+SEMAPHORES = (["wl", "xl", "ms", "ids", "sent", "st0", "st1"]
+              + ["%s%d" % (s, k) for s in ("wa", "xa", "v2m", "v2c", "v3m", "v3c", "ym", "yc") for k in range(N)]
+              + ["%s%d_%d" % (s, k, i) for s in ("tr", "wc") for k in range(N) for i in range(DEG)])
 
 
 def _bits(m):
     return [b for b in range(m.bit_length()) if (m >> b) & 1]
 
 
-def _mask_of(bs):
-    m = 0
-    for b in bs:
-        m |= 1 << b
-    return m
-
-
-def _share(engines, parts):
-    per = len(engines) // parts
+def _deal(mask, dsts):
+    if not dsts:
+        return {}
+    eng = _bits(mask)
+    per = len(eng) // len(dsts)
     per = 1 << (per.bit_length() - 1)
-    return [_mask_of(engines[t * per:(t + 1) * per]) for t in range(parts)]
+    return {j: sum(1 << b for b in eng[t * per:(t + 1) * per]) for t, j in enumerate(dsts)}
 
 
-def _same_chip(topo, a, b):
-    return topo.host(a) == topo.host(b) and topo.chip(a) == topo.chip(b)
+def _place(topo, c):
+    return (topo.host(c), topo.chip(c))
 
 
-def _plan(topo, cores, src):
-    c = cores[src]
-    near = [j for j in range(len(cores)) if j != src and _same_chip(topo, cores[j], c)]
-    far = [j for j in range(len(cores)) if j != src and not _same_chip(topo, cores[j], c)]
-    masks = {}
-    off = 0
-    if far:
-        off = topo.mask(c, cores[far[0]])
+def _routes(topo, cores, MASK):
+    n = len(cores)
+    out = []
+    for s in range(n):
+        c = cores[s]
+        near = [j for j in range(n) if j != s and _place(topo, cores[j]) == _place(topo, c)]
+        far = sorted([j for j in range(n) if j != s and j not in near], key=lambda j: 0 if s in MASK[j] else 1)
+        groups = {}
         for j in far:
-            off &= topo.mask(c, cores[j])
-        for j, m in zip(far, _share(_bits(off), len(far))):
-            masks[j] = m
-    if near:
-        on = topo.mask(c, cores[near[0]])
-        for j in near:
-            on &= topo.mask(c, cores[j])
-        rest = on & ~off
-        for j, m in zip(near, _share(_bits(rest if rest else on), len(near))):
-            masks[j] = m
-    return near, far, masks
+            groups.setdefault(_place(topo, cores[j]), []).append(j)
+        d = {"near": near, "far": far, "hx": [], "tx": {}}
+        for key in sorted(groups):
+            hx = ([j for j in groups[key] if topo.die(cores[j]) == topo.die(c)] or groups[key])[0]
+            d["hx"].append(hx)
+            d["tx"][hx] = [j for j in groups[key] if j != hx]
+        off = on = 0
+        for t, j in enumerate(far):
+            off = topo.mask(c, cores[j]) if t == 0 else off & topo.mask(c, cores[j])
+        for t, j in enumerate(near):
+            on = topo.mask(c, cores[j]) if t == 0 else on & topo.mask(c, cores[j])
+        d["off"], d["on"], d["side"] = off, on, (on & ~off) or on
+        out.append(d)
+    return out
 
 
 def rank_program(g, core, T, topo):
@@ -78,11 +71,26 @@ def rank_program(g, core, T, topo):
         return
     MASK, cores, S = T.tables["MASK"], T.cores, T.sem
     pe, ve, sy, sc = g.tensor, g.vector, g.sync, g.scalar
-    near, far, mine = _plan(topo, cores, r)
-    order = [r] + near + sorted(far, key=lambda j: 0 if j in MASK[r] else 1)
+    routes = _routes(topo, cores, MASK)
+    me = routes[r]
+    near = me["near"]
+    far = sorted(me["far"], key=lambda s: 0 if s in MASK[r] else 1)
+    xdir = [s for s in far if r in routes[s]["hx"]]
+    order = [r] + near + far
+    xorder = [r] + near + xdir + [s for s in far if s not in xdir]
+    pos = {k: n for n, k in enumerate(order)}
+    local = [r] + near
 
-    def engines(src):
-        return len(_bits(_plan(topo, cores, src)[2][r]))
+    def arrives(k, what):
+        d = routes[k]
+        if r in d["near"]:
+            return len(_bits(_deal(d["side"], d["near"])[r]))
+        if what == "w":
+            return len(_bits(d["off"]))
+        if r in d["hx"]:
+            return len(_bits(_deal(d["off"], d["hx"])[r]))
+        h = [h for h in d["hx"] if r in d["tx"][h]][0]
+        return len(_bits(_deal(routes[h]["on"], d["tx"][h])[r]))
 
     def wtile(buf, k, i):
         return buf[:, k * WC + i * P:k * WC + (i + 1) * P]
@@ -92,122 +100,133 @@ def rank_program(g, core, T, topo):
 
     sy.dma_start(T.wb[:, r * WC:(r + 1) * WC], T.w[:]).then_inc(S.wl, 16)
     sy.dma_start(T.xb[:, r * TK:(r + 1) * TK], T.x[:]).then_inc(S.xl, 16)
-    ve.memset(T.z[:], 0.0).then_inc(S.ms, 1)
-    ve.wait_ge(S.ms, 1)
-    ve.memset(T.z[:, 0:1], 1.0).then_inc(S.ms, 1)
-    sc.wait_ge(S.ms, 2)
-    sc.dma_start(T.idd[0], T.z[:]).then_inc(S.idw, 16)
-    sc.wait_ge(S.idw, 16)
-    sc.dma_start(T.idn[:], T.idd[0, 0:P * P]).then_inc(S.idr, 16)
+    ve.memset(T.one[:], 1.0).then_inc(S.ms, 1)
+    g.wait_ge(S.ms, 1)
+    g.affine_select(out=T.idn[:], in_=T.one[:], pattern=[[-1, P]], compare_op=AluOpType.is_equal, fill=0.0, base=0,
+                    channel_multiplier=1).then_inc(S.ids, 1)
 
     sent = [0]
 
-    def send(dsts, buf, width, sem):
-        if not dsts:
+    def send(buf, src, width, sem, masks):
+        if not masks:
             return
-        ap = buf[:, r * width:(r + 1) * width]
+        ap = buf[:, src * width:(src + 1) * width]
         trs = []
-        for j in dsts:
+        for j in masks:
             rid, pid = topo.addr(cores[j], core)
-            trs.append(RemoteDMATransfer(dst_ids=[DstId(rid=rid, pnc=pid)], dma_engine_mask=mine[j], remote_sem=sem,
+            trs.append(RemoteDMATransfer(dst_ids=[DstId(rid=rid, pnc=pid)], dma_engine_mask=masks[j], remote_sem=sem,
                                          src=ap, dst=ap))
-            sent[0] += len(_bits(mine[j]))
+            sent[0] += len(_bits(masks[j]))
         g.remote_dma_fused(trs, local_sem=S.sent)
 
     g.wait_ge(S.wl, 16)
-    send(far, T.wb, WC, S["wa%d" % r])
-    send(near, T.wb, WC, S["wa%d" % r])
+    send(T.wb, r, WC, S["wa%d" % r], _deal(me["side"], near))
+    for i in range(DEG):
+        g.wait_ge(S["wc%d_%d" % (r, i)], 1)
+    for j in me["far"]:
+        send(T.wt, r, WC, S["wa%d" % r], {j: me["off"]})
     g.wait_ge(S.xl, 16)
-    send(far, T.xb, TK, S["xa%d" % r])
-    send(near, T.xb, TK, S["xa%d" % r])
+    if me["off"] & me["side"]:
+        send(T.xb, r, TK, S["xa%d" % r], _deal(me["off"], me["hx"]))
+        send(T.xb, r, TK, S["xa%d" % r], _deal(me["side"], near))
+    else:
+        both = _deal(me["off"], me["hx"])
+        both.update(_deal(me["side"], near))
+        send(T.xb, r, TK, S["xa%d" % r], both)
+    for s in xdir:
+        g.wait_ge(S["xa%d" % s], arrives(s, "x"))
+        send(T.xb, s, TK, S["xa%d" % s], _deal(me["on"], routes[s]["tx"][r]))
     g.wait_ge(S.sent, sent[0])
 
-    t2 = [(MASK[k][i2], k, i1, i2) for k in order for i1 in range(DEG) if MASK[r][i1] == k for i2 in range(DEG)]
-    n2 = [sum(1 for t in t2 if t[0] == j) for j in range(N)]
-    t3 = {j: [(l, i) for l in order if n2[l] for i in range(DEG) if MASK[l][i] == j] for j in range(N)}
-    last2 = {t[0]: t[1] for t in t2}
-    early = order[:1 + len(near)]
-    bank = {k: (T.tra, T.trb)[n % 2] for n, k in enumerate(order)}
+    lpref = [r] + far + near
+    t2 = {k: sorted([(MASK[k][i2], i1, i2) for i1 in range(DEG) if MASK[r][i1] == k for i2 in range(DEG)],
+                    key=lambda t: lpref.index(t[0])) for k in order}
+    n2 = [sum(1 for k in order for t in t2[k] if t[0] == l) for l in range(N)]
+    shut2 = {l: max(pos[k] for k in order for t in t2[k] if t[0] == l) for l in range(N) if n2[l]}
+    ready = {l: max(shut2[l], pos[l]) for l in shut2}
+    n3 = [sum(1 for l in ready for i in range(DEG) if MASK[l][i] == j) for j in range(N)]
+    shut3 = {j: max(ready[l] for l in ready if j in MASK[l]) for j in range(N) if n3[j]}
+    ys_of = sorted([j for j in range(N) if n3[j]], key=lambda j: (shut3[j], xorder.index(j)))
 
-    def have_w(k):
-        if k == r:
-            pe.wait_ge(S.wl, 16)
+    turn = [0]
+
+    def copy(out, in_, sem, count, done, eng=None):
+        e = turn[0] % 2 if eng is None else eng
+        turn[0] += 1
+        if e == 0:
+            ve.wait_ge(sem, count)
+            ve.tensor_copy(out=out, in_=in_).then_inc(done, 1)
         else:
-            pe.wait_ge(S["wa%d" % k], engines(k))
+            sc.wait_ge(sem, count)
+            sc.activation(out=out, in_=in_, func=ActivationFunctionType.Copy).then_inc(done, 1)
 
-    def have_x(j):
-        if j == r:
-            pe.wait_ge(S.xl, 16)
-        else:
-            pe.wait_ge(S["xa%d" % j], engines(j))
+    free = [("k%d" % n, None) for n in range(NBANK)]
 
-    def transpose(k):
-        have_w(k)
-        for i in range(DEG):
-            pe.matmul(out=blk(bank[k], i), lhsT=wtile(T.wb, k, i), rhs=T.idn[:], start=True, stop=True
-                      ).then_inc(S["tr%d" % k], 1)
+    def take():
+        name, emptied = free.pop(0)
+        if emptied is not None:
+            pe.wait_ge(emptied, 1)
+        return blk(T[name], 0), name
 
-    seen2 = [0] * N
+    have = []
 
-    def v2_terms(k):
-        pe.wait_ge(S["wt%d" % k], 1)
-        for (j, kk, i1, i2) in t2:
-            if kk != k:
-                continue
-            seen2[j] += 1
-            pe.matmul(out=blk(T["p%d" % j], 0), lhsT=wtile(T.wt, k, i2), rhs=wtile(T.wb, r, i1),
-                      start=(seen2[j] == 1), stop=(seen2[j] == n2[j])).then_inc(S["v2m%d" % j], 1)
+    def wT(k, i):
+        if k in local and (k, i) not in have:
+            pe.wait_ge(S["wc%d_%d" % (k, i)], 1)
+            have.append((k, i))
+        return wtile(T.wt, k, i)
 
-    pe.wait_ge(S.idr, 16)
-    for k in early:
-        transpose(k)
-    for k in early:
-        v2_terms(k)
-    for k in order[len(early):]:
-        transpose(k)
-    for k in order[len(early):]:
-        v2_terms(k)
-    for j in range(N):
-        if n2[j]:
-            pe.wait_ge(S["v2c%d" % j], 1)
-    for j in order:
-        for n, (l, i) in enumerate(t3[j]):
-            pe.matmul(out=blk(T["p%d" % j], 0), lhsT=wtile(T.wt, l, i), rhs=blk(T.v2, l),
-                      start=(n == 0), stop=(n == len(t3[j]) - 1)).then_inc(S["v3m%d" % j], 1)
-    for n, j in enumerate(order):
+    b2, b3, by = {}, {}, {}
+    seen2, seen3 = [0] * N, [0] * N
+    pe.wait_ge(S.ids, 1)
+    for p, k in enumerate(order):
+        pe.wait_ge(S.wl, 16) if k == r else pe.wait_ge(S["wa%d" % k], arrives(k, "w"))
+        if k in local:
+            first = [t[2] for t in t2[k]]
+            for i in first + [i for i in range(DEG) if i not in first]:
+                ap, name = take()
+                pe.matmul(out=ap, lhsT=wtile(T.wb, k, i), rhs=T.idn[:], start=True, stop=True
+                          ).then_inc(S["tr%d_%d" % (k, i)], 1)
+                copy(wtile(T.wt, k, i), ap, S["tr%d_%d" % (k, i)], 1, S["wc%d_%d" % (k, i)])
+                free.append((name, S["wc%d_%d" % (k, i)]))
+        for (l, i1, i2) in t2[k]:
+            if l not in b2:
+                b2[l] = take()
+            seen2[l] += 1
+            pe.matmul(out=b2[l][0], lhsT=wT(k, i2), rhs=wtile(T.wb, r, i1),
+                      start=(seen2[l] == 1), stop=(seen2[l] == n2[l])).then_inc(S["v2m%d" % l], 1)
+            if seen2[l] == n2[l]:
+                copy(blk(T.v2, l), b2[l][0], S["v2m%d" % l], n2[l], S["v2c%d" % l])
+                free.append((b2[l][1], S["v2c%d" % l]))
+        t3 = [(l, i, MASK[l][i]) for l in lpref if l in ready and ready[l] == p for i in range(DEG)]
+        t3.sort(key=lambda t: (shut3[t[2]] != p, ys_of.index(t[2])))
+        waited = []
+        for (l, i, j) in t3:
+            if l not in waited:
+                pe.wait_ge(S["v2c%d" % l], 1)
+                waited.append(l)
+            if j not in b3:
+                b3[j] = take()
+            seen3[j] += 1
+            pe.matmul(out=b3[j][0], lhsT=wT(l, i), rhs=blk(T.v2, l),
+                      start=(seen3[j] == 1), stop=(seen3[j] == n3[j])).then_inc(S["v3m%d" % j], 1)
+            if seen3[j] == n3[j]:
+                copy(blk(T.v3, j), b3[j][0], S["v3m%d" % j], n3[j], S["v3c%d" % j])
+                free.append((b3[j][1], S["v3c%d" % j]))
+    for n, j in enumerate(ys_of):
         pe.wait_ge(S["v3c%d" % j], 1)
-        have_x(j)
-        for h in range(NH):
-            pe.matmul(out=T["y%d" % h][:, 0:HW], lhsT=blk(T.v3, j), rhs=T.xb[:, j * TK + h * HW:j * TK + (h + 1) * HW],
-                      start=(n == 0), stop=(n == N - 1)).then_inc(S["ym%d" % h], 1)
+        pe.wait_ge(S.xl, 16) if j == r else pe.wait_ge(S["xa%d" % j], arrives(j, "x"))
+        for q in range(NQ):
+            if q not in by:
+                by[q] = take()
+            pe.matmul(out=by[q][0], lhsT=blk(T.v3, j), rhs=T.xb[:, j * TK + q * P:j * TK + (q + 1) * P],
+                      start=(n == 0), stop=(n == len(ys_of) - 1)).then_inc(S["ym%d" % q], 1)
+    for q in range(NQ):
+        copy(blk(T.ys, q), by[q][0], S["ym%d" % q], len(ys_of), S["yc%d" % q], eng=(q + 1) % 2)
 
-    def wt_copy(k):
-        ve.wait_ge(S["tr%d" % k], DEG)
-        ve.tensor_copy(out=T.wt[:, k * WC:(k + 1) * WC], in_=bank[k][:, 0:WC]).then_inc(S["wt%d" % k], 1)
-
-    def v2_copy(j):
-        ve.wait_ge(S["v2m%d" % j], n2[j])
-        ve.tensor_copy(out=blk(T.v2, j), in_=blk(T["p%d" % j], 0)).then_inc(S["v2c%d" % j], 1)
-
-    for k in early:
-        wt_copy(k)
-    for j in order:
-        if n2[j] and last2[j] in early:
-            v2_copy(j)
-    for k in order[len(early):]:
-        wt_copy(k)
-    for j in order:
-        if n2[j] and last2[j] not in early:
-            v2_copy(j)
-    for j in order:
-        ve.wait_ge(S["v3m%d" % j], len(t3[j]))
-        ve.tensor_copy(out=blk(T.v3, j), in_=blk(T["p%d" % j], 0)).then_inc(S["v3c%d" % j], 1)
-    for h in range(NH):
-        ve.wait_ge(S["ym%d" % h], N)
-        ve.tensor_copy(out=T.ys[:, h * HW:(h + 1) * HW], in_=T["y%d" % h][:, 0:HW]).then_inc(S["yc%d" % h], 1)
-
-    for h in range(NH):
-        q = (sy, sc)[h % 2]
-        q.wait_ge(S["yc%d" % h], 1)
-        q.dma_start(T.y[:, h * HW:(h + 1) * HW], T.ys[:, h * HW:(h + 1) * HW]).then_inc(S["st%d" % h], 16)
+    HQ = NQ // 2
+    for h, q in enumerate((sy, sc)):
+        for n in range(h * HQ, (h + 1) * HQ):
+            q.wait_ge(S["yc%d" % n], 1)
+        q.dma_start(T.y[:, h * HQ * P:(h + 1) * HQ * P], T.ys[:, h * HQ * P:(h + 1) * HQ * P]).then_inc(S["st%d" % h], 16)
         q.wait_ge(S["st%d" % h], 16)

from concourse.bass import DstId, RemoteDMATransfer
from concourse.mybir import AluOpType, ActivationFunctionType

N, DEG, P, TK = 4, 3, 128, 512
WC = DEG * P
NQ = TK // P
NBANK = 8

SCRATCH = {
    "wb": ("sbuf", [P, N * WC], "bfloat16"),
    "xb": ("sbuf", [P, N * TK], "bfloat16"),
    "wt": ("sbuf", [P, N * WC], "bfloat16"),
    "v2": ("sbuf", [P, N * P], "bfloat16"),
    "v3": ("sbuf", [P, N * P], "bfloat16"),
    "ys": ("sbuf", [P, TK], "bfloat16"),
    "one": ("sbuf", [P, P], "bfloat16"),
    "idn": ("sbuf", [P, P], "bfloat16"),
}
for _n in range(NBANK):
    SCRATCH["k%d" % _n] = ("psum", [P, 512], "float32")
SEMAPHORES = (["wl", "xl", "ms", "ids", "sent", "st0", "st1"]
              + ["%s%d" % (s, k) for s in ("wa", "xa", "v2m", "v2c", "v3m", "v3c", "ym", "yc") for k in range(N)]
              + ["%s%d_%d" % (s, k, i) for s in ("tr", "wc") for k in range(N) for i in range(DEG)])


def _bits(m):
    return [b for b in range(m.bit_length()) if (m >> b) & 1]


def _deal(mask, dsts):
    if not dsts:
        return {}
    eng = _bits(mask)
    per = len(eng) // len(dsts)
    per = 1 << (per.bit_length() - 1)
    return {j: sum(1 << b for b in eng[t * per:(t + 1) * per]) for t, j in enumerate(dsts)}


def _place(topo, c):
    return (topo.host(c), topo.chip(c))


def _routes(topo, cores, MASK):
    n = len(cores)
    out = []
    for s in range(n):
        c = cores[s]
        near = [j for j in range(n) if j != s and _place(topo, cores[j]) == _place(topo, c)]
        far = sorted([j for j in range(n) if j != s and j not in near], key=lambda j: 0 if s in MASK[j] else 1)
        groups = {}
        for j in far:
            groups.setdefault(_place(topo, cores[j]), []).append(j)
        d = {"near": near, "far": far, "hx": [], "tx": {}}
        for key in sorted(groups):
            hx = ([j for j in groups[key] if topo.die(cores[j]) == topo.die(c)] or groups[key])[0]
            d["hx"].append(hx)
            d["tx"][hx] = [j for j in groups[key] if j != hx]
        off = on = 0
        for t, j in enumerate(far):
            off = topo.mask(c, cores[j]) if t == 0 else off & topo.mask(c, cores[j])
        for t, j in enumerate(near):
            on = topo.mask(c, cores[j]) if t == 0 else on & topo.mask(c, cores[j])
        d["off"], d["on"], d["side"] = off, on, (on & ~off) or on
        out.append(d)
    return out


def rank_program(g, core, T, topo):
    r = T.rank_of(core)
    if r is None:
        return
    MASK, cores, S = T.tables["MASK"], T.cores, T.sem
    pe, ve, sy, sc = g.tensor, g.vector, g.sync, g.scalar
    routes = _routes(topo, cores, MASK)
    me = routes[r]
    near = me["near"]
    far = sorted(me["far"], key=lambda s: 0 if s in MASK[r] else 1)
    xdir = [s for s in far if r in routes[s]["hx"]]
    order = [r] + near + far
    xorder = [r] + near + xdir + [s for s in far if s not in xdir]
    pos = {k: n for n, k in enumerate(order)}
    local = [r] + near

    def arrives(k, what):
        d = routes[k]
        if r in d["near"]:
            return len(_bits(_deal(d["side"], d["near"])[r]))
        if what == "w":
            return len(_bits(d["off"]))
        if r in d["hx"]:
            return len(_bits(_deal(d["off"], d["hx"])[r]))
        h = [h for h in d["hx"] if r in d["tx"][h]][0]
        return len(_bits(_deal(routes[h]["on"], d["tx"][h])[r]))

    def wtile(buf, k, i):
        return buf[:, k * WC + i * P:k * WC + (i + 1) * P]

    def blk(buf, j):
        return buf[:, j * P:(j + 1) * P]

    sy.dma_start(T.wb[:, r * WC:(r + 1) * WC], T.w[:]).then_inc(S.wl, 16)
    sy.dma_start(T.xb[:, r * TK:(r + 1) * TK], T.x[:]).then_inc(S.xl, 16)
    ve.memset(T.one[:], 1.0).then_inc(S.ms, 1)
    g.wait_ge(S.ms, 1)
    g.affine_select(out=T.idn[:], in_=T.one[:], pattern=[[-1, P]], compare_op=AluOpType.is_equal, fill=0.0, base=0,
                    channel_multiplier=1).then_inc(S.ids, 1)

    sent = [0]

    def send(buf, src, width, sem, masks):
        if not masks:
            return
        ap = buf[:, src * width:(src + 1) * width]
        trs = []
        for j in masks:
            rid, pid = topo.addr(cores[j], core)
            trs.append(RemoteDMATransfer(dst_ids=[DstId(rid=rid, pnc=pid)], dma_engine_mask=masks[j], remote_sem=sem,
                                         src=ap, dst=ap))
            sent[0] += len(_bits(masks[j]))
        g.remote_dma_fused(trs, local_sem=S.sent)

    g.wait_ge(S.wl, 16)
    send(T.wb, r, WC, S["wa%d" % r], _deal(me["side"], near))
    for i in range(DEG):
        g.wait_ge(S["wc%d_%d" % (r, i)], 1)
    for j in me["far"]:
        send(T.wt, r, WC, S["wa%d" % r], {j: me["off"]})
    g.wait_ge(S.xl, 16)
    if me["off"] & me["side"]:
        send(T.xb, r, TK, S["xa%d" % r], _deal(me["off"], me["hx"]))
        send(T.xb, r, TK, S["xa%d" % r], _deal(me["side"], near))
    else:
        both = _deal(me["off"], me["hx"])
        both.update(_deal(me["side"], near))
        send(T.xb, r, TK, S["xa%d" % r], both)
    for s in xdir:
        g.wait_ge(S["xa%d" % s], arrives(s, "x"))
        send(T.xb, s, TK, S["xa%d" % s], _deal(me["on"], routes[s]["tx"][r]))
    g.wait_ge(S.sent, sent[0])

    lpref = [r] + far + near
    t2 = {k: sorted([(MASK[k][i2], i1, i2) for i1 in range(DEG) if MASK[r][i1] == k for i2 in range(DEG)],
                    key=lambda t: lpref.index(t[0])) for k in order}
    n2 = [sum(1 for k in order for t in t2[k] if t[0] == l) for l in range(N)]
    shut2 = {l: max(pos[k] for k in order for t in t2[k] if t[0] == l) for l in range(N) if n2[l]}
    ready = {l: max(shut2[l], pos[l]) for l in shut2}
    n3 = [sum(1 for l in ready for i in range(DEG) if MASK[l][i] == j) for j in range(N)]
    shut3 = {j: max(ready[l] for l in ready if j in MASK[l]) for j in range(N) if n3[j]}
    ys_of = sorted([j for j in range(N) if n3[j]], key=lambda j: (shut3[j], xorder.index(j)))

    turn = [0]

    def copy(out, in_, sem, count, done, eng=None):
        e = turn[0] % 2 if eng is None else eng
        turn[0] += 1
        if e == 0:
            ve.wait_ge(sem, count)
            ve.tensor_copy(out=out, in_=in_).then_inc(done, 1)
        else:
            sc.wait_ge(sem, count)
            sc.activation(out=out, in_=in_, func=ActivationFunctionType.Copy).then_inc(done, 1)

    free = [("k%d" % n, None) for n in range(NBANK)]

    def take():
        name, emptied = free.pop(0)
        if emptied is not None:
            pe.wait_ge(emptied, 1)
        return blk(T[name], 0), name

    have = []

    def wT(k, i):
        if k in local and (k, i) not in have:
            pe.wait_ge(S["wc%d_%d" % (k, i)], 1)
            have.append((k, i))
        return wtile(T.wt, k, i)

    b2, b3, by = {}, {}, {}
    seen2, seen3 = [0] * N, [0] * N
    pe.wait_ge(S.ids, 1)
    for p, k in enumerate(order):
        pe.wait_ge(S.wl, 16) if k == r else pe.wait_ge(S["wa%d" % k], arrives(k, "w"))
        if k in local:
            first = [t[2] for t in t2[k]]
            for i in first + [i for i in range(DEG) if i not in first]:
                ap, name = take()
                pe.matmul(out=ap, lhsT=wtile(T.wb, k, i), rhs=T.idn[:], start=True, stop=True
                          ).then_inc(S["tr%d_%d" % (k, i)], 1)
                copy(wtile(T.wt, k, i), ap, S["tr%d_%d" % (k, i)], 1, S["wc%d_%d" % (k, i)])
                free.append((name, S["wc%d_%d" % (k, i)]))
        for (l, i1, i2) in t2[k]:
            if l not in b2:
                b2[l] = take()
            seen2[l] += 1
            pe.matmul(out=b2[l][0], lhsT=wT(k, i2), rhs=wtile(T.wb, r, i1),
                      start=(seen2[l] == 1), stop=(seen2[l] == n2[l])).then_inc(S["v2m%d" % l], 1)
            if seen2[l] == n2[l]:
                copy(blk(T.v2, l), b2[l][0], S["v2m%d" % l], n2[l], S["v2c%d" % l])
                free.append((b2[l][1], S["v2c%d" % l]))
        t3 = [(l, i, MASK[l][i]) for l in lpref if l in ready and ready[l] == p for i in range(DEG)]
        t3.sort(key=lambda t: (shut3[t[2]] != p, ys_of.index(t[2])))
        waited = []
        for (l, i, j) in t3:
            if l not in waited:
                pe.wait_ge(S["v2c%d" % l], 1)
                waited.append(l)
            if j not in b3:
                b3[j] = take()
            seen3[j] += 1
            pe.matmul(out=b3[j][0], lhsT=wT(l, i), rhs=blk(T.v2, l),
                      start=(seen3[j] == 1), stop=(seen3[j] == n3[j])).then_inc(S["v3m%d" % j], 1)
            if seen3[j] == n3[j]:
                copy(blk(T.v3, j), b3[j][0], S["v3m%d" % j], n3[j], S["v3c%d" % j])
                free.append((b3[j][1], S["v3c%d" % j]))
    for n, j in enumerate(ys_of):
        pe.wait_ge(S["v3c%d" % j], 1)
        pe.wait_ge(S.xl, 16) if j == r else pe.wait_ge(S["xa%d" % j], arrives(j, "x"))
        for q in range(NQ):
            if q not in by:
                by[q] = take()
            pe.matmul(out=by[q][0], lhsT=blk(T.v3, j), rhs=T.xb[:, j * TK + q * P:j * TK + (q + 1) * P],
                      start=(n == 0), stop=(n == len(ys_of) - 1)).then_inc(S["ym%d" % q], 1)
    for q in range(NQ):
        copy(blk(T.ys, q), by[q][0], S["ym%d" % q], len(ys_of), S["yc%d" % q], eng=(q + 1) % 2)

    HQ = NQ // 2
    for h, q in enumerate((sy, sc)):
        for n in range(h * HQ, (h + 1) * HQ):
            q.wait_ge(S["yc%d" % n], 1)
        q.dma_start(T.y[:, h * HQ * P:(h + 1) * HQ * P], T.ys[:, h * HQ * P:(h + 1) * HQ * P]).then_inc(S["st%d" % h], 16)
        q.wait_ge(S["st%d" % h], 16)
